import numpy as np, ml_dtypes
CORES = [24,26,29,31,48,50,53,55]
N = 8
import mx_ref
NC, G, MB = 128, 4, 4
C = np.float32(0.037)
BF = ml_dtypes.bfloat16
def cut(t, i, w=512):
    return t[:, w * i:w * i + w]
def tile(rs):
    return np.stack(rs, axis=2).reshape(128, -1).astype(BF)
def layer(w, X):
    out = []
    for i in range(G):
        for t in range(len(X)):
            p = mx_ref.matmul(mx_ref.quantize(cut(w, len(X) * i + t)), X[t])
            z = p if t == 0 else z + p
        out.append(z)
    return out
def act(Z):
    return [np.maximum(z, 0) * C for z in Z]
def masked(U, Z):
    return [(u * (z > 0)) * C for u, z in zip(U, Z)]
def setup_inputs(rng):
    def f(*shape):
        return mx_ref.flush((rng.standard_normal(shape, dtype=np.float32) * np.exp2(rng.integers(-2, 3, shape[:-1] + (1,)))).astype(BF))
    return {"x": f(N, 128, MB * 4 * NC), "e": f(N, 128, MB * 4 * NC), "w": f(N, 128, G * 512), "v": f(N, 128, G * 512)}
def setup_inputs_blocks(rng):
    d = setup_inputs(rng)
    for k in ("x", "e"): d[k] = mx_ref.spread(d[k], rng, 4)
    for k in ("w", "v"): d[k] = mx_ref.spread(d[k], rng, 1)
    return d
def setup_inputs_wide(rng):
    d = setup_inputs(rng)
    for k in ("x", "e"): d[k] = mx_ref.flush((d[k].astype(np.float32) * np.exp2(rng.integers(-8, 9, (N, 1, 1))).astype(np.float32)).astype(BF))
    return d
def setup_inputs_zeros(rng):
    d = setup_inputs(rng); v = d["x"].reshape(N, 128, -1, 4).copy()
    v[np.broadcast_to((rng.random((N, 1, v.shape[2], 1)) < 0.33), v.shape)] = 0
    d["x"] = v.reshape(d["x"].shape)
    return d
def reference(x, e, w, v):
    y = np.full((N, 128, MB * G * NC), np.nan, np.float32)
    for m in range(MB):
        a = mx_ref.quantize(cut(x[N - 1], m, 4 * NC)); Z = []
        for s in range(N):
            Z.append(layer(w[s], [a]))
            if s < N - 1: a = mx_ref.quantize(tile(act(Z[s])))
        b = mx_ref.quantize(cut(e[0], m, 4 * NC))
        for s in range(N - 1, 0, -1):
            b = mx_ref.quantize(tile(masked(layer(v[s], [b]), Z[s])))
        U = layer(v[0], [b])
        for i in range(G):
            y[0][:, NC * (G * m + i):NC * (G * m + i) + NC] = U[i] * (Z[0][i] > 0)
    return {"y": y}

@@ -1,0 +1,277 @@
+from concourse.bass import DstId, RemoteDMATransfer
+from concourse.mybir import dt, AluOpType, ActivationFunctionType
+
+C = 0.037
+NT, W, NCORES = 4, 128, 64
+
+SCRATCH = {
+    "ps": ("psum", [128, 4096], "float32"),
+    "xin": ("sbuf", [128, 2048], "bfloat16"),
+    "ein": ("sbuf", [128, 2048], "bfloat16"),
+    "win": ("sbuf", [128, 2048], "bfloat16"),
+    "vin": ("sbuf", [128, 2048], "bfloat16"),
+    "wc": ("sbuf", [128, 512], "float8_e4m3fn_x4"), "wp": ("sbuf", [128, 512], "uint8"),
+    "vc": ("sbuf", [128, 512], "float8_e4m3fn_x4"), "vp": ("sbuf", [128, 512], "uint8"),
+    "xc": ("sbuf", [128, 512], "float8_e4m3fn_x4"), "xp": ("sbuf", [128, 512], "uint8"),
+    "ec": ("sbuf", [128, 512], "float8_e4m3fn_x4"), "ep": ("sbuf", [128, 512], "uint8"),
+    "ac": ("sbuf", [128, 512], "float8_e4m3fn_x4"), "ap": ("sbuf", [128, 512], "uint8"),
+    "bc": ("sbuf", [128, 512], "float8_e4m3fn_x4"), "bp": ("sbuf", [128, 512], "uint8"),
+    "dc": ("sbuf", [128, 512], "float8_e4m3fn_x4"), "dp": ("sbuf", [128, 512], "uint8"),
+    "uc": ("sbuf", [128, 512], "float8_e4m3fn_x4"), "up": ("sbuf", [128, 512], "uint8"),
+    "rc": ("sbuf", [128, 512], "float8_e4m3fn_x4"), "rp": ("sbuf", [128, 512], "uint8"),
+    "td": ("sbuf", [128, 2048], "bfloat16"),
+    "tb": ("sbuf", [128, 2048], "bfloat16"),
+    "mask": ("sbuf", [128, 2048], "float32"),
+    "sg": ("sbuf", [128, 2048], "float32"),
+    "yb": ("sbuf", [128, 2048], "float32"),
+}
+SEMAPHORES = (["ldw", "ldv", "lde", "wr", "vr", "eq", "xq", "pe", "va", "sa", "qz", "mk", "ls", "lx", "st0", "st1"]
+              + ["%s%d" % (k, m) for k in ("ldx", "ad", "ab", "re", "rb") for m in range(NT)])
+
+
+def _bits(mask):
+    return [1 << k for k in range(mask.bit_length()) if (mask >> k) & 1]
+
+
+def _plan(T, topo):
+    R = T.cores
+
+    def helper(near, far, die):
+        return [c for c in range(NCORES) if topo.chip(c) == topo.chip(near) and T.rank_of(c) is None
+                and topo.may_write(c, far) and topo.die(c) == die][0]
+    d0, d1 = topo.die(R[0]), topo.die(R[-1])
+    hA, hB = helper(R[0], R[7], d0), helper(R[0], R[7], d1)
+    kA, kB = helper(R[7], R[0], d0), helper(R[7], R[0], d1)
+    ways = [[R[0], hB, kB, R[7]],
+            [R[0], R[1], hA, kA, R[4], R[7]],
+            [R[0], R[2], hB, kB, R[6], R[7]],
+            [R[0], R[3], hA, kA, R[5], R[7]]]
+    return ways, kA, kB
+
+
+def rank_program(g, core, T, topo):
+    A = AluOpType
+    F = ActivationFunctionType
+    sem = T.sem
+    R = T.cores
+    N = len(R)
+    rank = T.rank_of(core)
+    ways, kA, kB = _plan(T, topo)
+    left = [0]
+
+    def n_eng(src, dst):
+        return len(_bits(topo.mask(src, dst)))
+
+    def cols(m, n=1):
+        return slice(W * m, W * (m + n))
+
+    def send(dst, out_ap, in_ap, rsem, lsem=None):
+        mask = topo.mask(core, dst)
+        rid, pid, _ = topo.addr(dst)
+        if lsem is None:
+            lsem = sem["ls"]
+            left[0] += len(_bits(mask))
+        g.remote_dma(out_ap, in_ap, rsem, lsem, pid, rid, mask)
+
+    def send_codes(dst, dbuf, sbuf, m, rsem, lsem=None):
+        send(dst, T[dbuf][:, cols(m)].bitcast(dt.uint8), T[sbuf][:, cols(m)].bitcast(dt.uint8), rsem, lsem)
+
+    def send_scales(dst, dbuf, sbuf, m, rsem, lsem=None):
+        send(dst, T[dbuf][:, cols(m)], T[sbuf][:, cols(m)], rsem, lsem)
+
+    def relay_e():
+        for m in range(NT):
+            if core not in ways[m][1:-1]:
+                continue
+            k = ways[m].index(core)
+            before, after, final = ways[m][k - 1], ways[m][k + 1], k + 2 == len(ways[m])
+            rs = sem["ab%d" % m] if final else sem["re%d" % m]
+            g.wait_ge(sem["re%d" % m], 2 * (n_eng(before, core) // (NT if k == 1 else 1)))
+            send_codes(after, "bc" if final else "ec", "ec", m, rs)
+            send_scales(after, "bp" if final else "ep", "ep", m, rs)
+
+    def finish():
+        if left[0]:
+            g.wait_ge(sem["ls"], left[0])
+
+    if rank is None:
+        relay_e()
+        if core in (kA, kB):
+            for m in range(NT):
+                g.wait_ge(sem["rb%d" % m], n_eng(R[4], core))
+                if core == kA:
+                    send_codes(R[3], "bc", "rc", m, sem["ab%d" % m])
+                else:
+                    send_scales(R[3], "bp", "rp", m, sem["ab%d" % m])
+        finish()
+        return
+
+    last = rank == N - 1
+    PE, V, S, Y = g.tensor, g.vector, g.scalar, g.sync
+
+    if last:
+        for m in range(NT):
+            q = Y if m % 2 == 0 else S
+            q.dma_start(T.xin[:, 512 * m:512 * m + 512], T.x[:, 512 * m:512 * m + 512]).then_inc(sem["ldx%d" % m], 16)
+        for q in (Y, S):
+            q.wait_ge(sem["lx"], NT * 2 * n_eng(core, R[0]))
+    if rank == 0:
+        Y.dma_start(T.ein[:], T.e[:]).then_inc(sem["lde"], 16)
+    (S if rank == 0 else Y).dma_start(T.win[:], T.w[:]).then_inc(sem["ldw"], 16)
+    (Y if rank == 0 else S).dma_start(T.vin[:], T.v[:]).then_inc(sem["ldv"], 16)
+
+    if rank == 0:
+        V.wait_ge(sem["lde"], 16)
+        V.quantize_mx(T.ec[:], T.ep[:], T.ein[:]).then_inc(sem["eq"], 1)
+    if last:
+        for m in range(NT):
+            V.wait_ge(sem["ldx%d" % m], 16)
+            V.quantize_mx(T.xc[:, cols(m)], T.xp[:, cols(m)], T.xin[:, 512 * m:512 * m + 512]).then_inc(sem["xq"], 1)
+    V.wait_ge(sem["ldw"], 16)
+    V.quantize_mx(T.wc[:], T.wp[:], T.win[:]).then_inc(sem["wr"], 1)
+    V.wait_ge(sem["ldv"], 16)
+    V.quantize_mx(T.vc[:], T.vp[:], T.vin[:]).then_inc(sem["vr"], 1)
+
+    if rank == 0:
+        g.wait_ge(sem["eq"], 1)
+        eng = _bits(topo.mask(core, ways[0][1]))
+        per = len(eng) // NT
+        for buf in ("ec", "ep"):
+            tr = []
+            for m in range(NT):
+                rid, pid, _ = topo.addr(ways[m][1])
+                src, dst = T[buf][:, cols(m)], T[buf][:, cols(m)]
+                if buf == "ec":
+                    src, dst = src.bitcast(dt.uint8), dst.bitcast(dt.uint8)
+                tr.append(RemoteDMATransfer(dst_ids=[DstId(rid=rid, pnc=pid)], dma_engine_mask=sum(eng[per * m:per * m + per]),
+                                            remote_sem=sem["re%d" % m], src=src, dst=dst))
+            g.remote_dma_fused(tr, local_sem=sem["ls"])
+            left[0] += len(eng)
+    if last:
+        for m in range(NT):
+            g.wait_ge(sem["xq"], m + 1)
+            send_codes(R[0], "ac", "xc", m, sem["ad%d" % m], sem["lx"])
+            send_scales(R[0], "ap", "xp", m, sem["ad%d" % m], sem["lx"])
+    relay_e()
+
+    n_down = 2 * n_eng(R[rank - 1], core)
+    if last:
+        back_arrive = [2 * n_eng(ways[m][-2], core) for m in range(NT)]
+    elif rank == 3:
+        back_arrive = [n_eng(kA, core) + n_eng(kB, core)] * NT
+    else:
+        back_arrive = [2 * n_eng(R[rank + 1], core)] * NT
+
+    def mm(bk, wts, i, src, m):
+        PE.matmul_mx(T.ps[:, 512 * bk:512 * bk + W], T[wts + "c"][:, cols(i)], T[wts + "p"][:, cols(i)],
+                     T[src + "c"][:, cols(m)], T[src + "p"][:, cols(m)], True, True).then_inc(sem["pe"], 1)
+
+    def bank(k):
+        return T.ps[:, 512 * k:512 * k + W]
+
+    def lane(buf, m, b):
+        return T[buf][:, 512 * m + b:512 * m + 512:4]
+
+    def quantise(m, codes, scales, tile):
+        V.quantize_mx(T[codes][:, cols(m)], T[scales][:, cols(m)], T[tile][:, 512 * m:512 * m + 512]).then_inc(sem["qz"], 1)
+
+    if last:
+        PE.wait_ge(sem["vr"], 1)
+        PE.wait_ge(sem["wr"], 1)
+        for m in range(NT):
+            PE.wait_ge(sem["ab%d" % m], back_arrive[m])
+            if m:
+                PE.wait_ge(sem["va"], 6 * m)
+                PE.wait_ge(sem["sa"], 4 * m)
+            for i in range(4):
+                mm(4 + i, "v", i, "b", m)
+            PE.wait_ge(sem["ad%d" % m], n_down)
+            for i in range(4):
+                mm(i, "w", i, "a", m)
+            p, v, s = 8 * m + 4, 6 * m, 4 * m
+            for k, b in enumerate((1, 2)):
+                S.wait_ge(sem["pe"], p + b + 1)
+                S.activation(lane("sg", m, b), bank(b), F.Sign).then_inc(sem["sa"], 1)
+                S.wait_ge(sem["sa"], s + 2 * k + 1)
+                S.activation(lane("mask", m, b), lane("sg", m, b), F.Relu, scale=C).then_inc(sem["sa"], 1)
+            for k, b in enumerate((0, 3)):
+                V.wait_ge(sem["pe"], p + b + 1)
+                V.tensor_scalar(lane("mask", m, b), bank(b), 0.0, C, A.is_gt, A.mult).then_inc(sem["va"], 1)
+                V.wait_ge(sem["va"], v + 2 * k + 1)
+                V.tensor_tensor(lane("tb", m, b), bank(4 + b), lane("mask", m, b), A.mult).then_inc(sem["va"], 1)
+            for k, b in enumerate((1, 2)):
+                V.wait_ge(sem["sa"], s + 2 * k + 2)
+                V.tensor_tensor(lane("tb", m, b), bank(4 + b), lane("mask", m, b), A.mult).then_inc(sem["va"], 1)
+            V.wait_ge(sem["va"], v + 6)
+            quantise(m, "uc", "up", "tb")
+    else:
+        jobs = [("d", m) for m in range(NT)] + [("b", m) for m in range(NT)]
+        va = sa = 0
+        done = []
+        for j, (way, m) in enumerate(jobs):
+            base = 4 * (j % 2)
+            p = 4 * j
+            if m == 0:
+                PE.wait_ge(sem["wr" if way == "d" else "vr"], 1)
+            PE.wait_ge(sem["a%s%d" % (way, m)], n_down if way == "d" else back_arrive[m])
+            if j >= 2:
+                PE.wait_ge(sem["va"], done[j - 2][0])
+                if jobs[j - 2][0] == "d":
+                    PE.wait_ge(sem["sa"], done[j - 2][1])
+            for i in range(4):
+                mm(base + i, "w" if way == "d" else "v", i, "a" if way == "d" else "b", m)
+            if way == "d":
+                for b in (1, 2):
+                    S.wait_ge(sem["pe"], p + b + 1)
+                    S.activation(lane("td", m, b), bank(base + b), F.Relu, scale=C).then_inc(sem["sa"], 1)
+                    sa += 1
+                for b in (0, 3):
+                    V.wait_ge(sem["pe"], p + b + 1)
+                    V.tensor_scalar(lane("td", m, b), bank(base + b), 0.0, C, A.max, A.mult).then_inc(sem["va"], 1)
+                    va += 1
+                V.wait_ge(sem["sa"], sa)
+                V.wait_ge(sem["va"], va)
+                quantise(m, "dc", "dp", "td")
+                t = slice(512 * m, 512 * m + 512)
+                if rank == 0:
+                    V.tensor_scalar(T.mask[:, t], T.td[:, t], 0.0, None, A.is_gt).then_inc(sem["mk"], 1)
+                else:
+                    V.tensor_scalar(T.mask[:, t], T.td[:, t], 0.0, C, A.is_gt, A.mult).then_inc(sem["mk"], 1)
+            else:
+                if m == 0:
+                    V.wait_ge(sem["mk"], NT)
+                for b in range(4):
+                    V.wait_ge(sem["pe"], p + b + 1)
+                    out = lane("tb", m, b) if rank else T.yb[:, cols(4 * m + b)]
+                    V.tensor_tensor(out, bank(base + b), lane("mask", m, b), A.mult).then_inc(sem["va"], 1)
+                    va += 1
+                    if rank == 0 and b % 2:
+                        q, st = ((Y, "st0"), (S, "st1"))[b // 2]
+                        q.wait_ge(sem["va"], va)
+                        q.dma_start(T.y[:, cols(4 * m + b - 1, 2)], T.yb[:, cols(4 * m + b - 1, 2)]).then_inc(sem[st], 16)
+                if rank:
+                    V.wait_ge(sem["va"], va)
+                    quantise(m, "uc", "up", "tb")
+            done.append((va, sa))
+        if rank == 0:
+            Y.wait_ge(sem["st0"], 16 * NT)
+            S.wait_ge(sem["st1"], 16 * NT)
+
+    n = 0
+    if not last:
+        for m in range(NT):
+            n += 1
+            g.wait_ge(sem["qz"], n)
+            send_codes(R[rank + 1], "ac", "dc", m, sem["ad%d" % m])
+            send_scales(R[rank + 1], "ap", "dp", m, sem["ad%d" % m])
+    if rank:
+        for m in range(NT):
+            n += 1
+            g.wait_ge(sem["qz"], n)
+            if rank == 4:
+                send_codes(kA, "rc", "uc", m, sem["rb%d" % m])
+                send_scales(kB, "rp", "up", m, sem["rb%d" % m])
+            else:
+                send_codes(R[rank - 1], "bc", "uc", m, sem["ab%d" % m])
+                send_scales(R[rank - 1], "bp", "up", m, sem["ab%d" % m])
+    finish()

@@ -1,4 +1,3 @@
-from concourse.bass import DstId, RemoteDMATransfer
 from concourse.mybir import dt, AluOpType, ActivationFunctionType
 
 C = 0.037
@@ -25,8 +24,8 @@ SCRATCH = {
     "sg": ("sbuf", [128, 2048], "float32"),
     "yb": ("sbuf", [128, 2048], "float32"),
 }
-SEMAPHORES = (["ldw", "ldv", "lde", "wr", "vr", "eq", "xq", "pe", "va", "sa", "qz", "mk", "ls", "lx", "st0", "st1"]
-              + ["%s%d" % (k, m) for k in ("ldx", "ad", "ab", "re", "rb") for m in range(NT)])
+SEMAPHORES = (["ldw", "ldv", "lde0", "lde1", "wr", "vr", "eq", "xq", "pe", "va", "sa", "qz", "mk", "ls", "lx", "st0", "st1"]
+              + ["%s%d" % (k, m) for k in ("ldx", "ad", "ab", "rec", "res", "rb") for m in range(NT)])
 
 
 def _bits(mask):
@@ -42,10 +41,10 @@ def _plan(T, topo):
     d0, d1 = topo.die(R[0]), topo.die(R[-1])
     hA, hB = helper(R[0], R[7], d0), helper(R[0], R[7], d1)
     kA, kB = helper(R[7], R[0], d0), helper(R[7], R[0], d1)
-    ways = [[R[0], hB, kB, R[7]],
-            [R[0], R[1], hA, kA, R[4], R[7]],
-            [R[0], R[2], hB, kB, R[6], R[7]],
-            [R[0], R[3], hA, kA, R[5], R[7]]]
+    ways = [[R[0], R[1], hA, R[5], R[7]],
+            [R[0], hA, R[4], kB, R[7]],
+            [R[0], R[2], hB, R[6], R[7]],
+            [R[0], R[3], hB, kA, R[7]]]
     return ways, kA, kB
 
 
@@ -79,16 +78,18 @@ def rank_program(g, core, T, topo):
     def send_scales(dst, dbuf, sbuf, m, rsem, lsem=None):
         send(dst, T[dbuf][:, cols(m)], T[sbuf][:, cols(m)], rsem, lsem)
 
+    def start_e(m):
+        g.wait_ge(sem["eq"], 2 if m else 1)
+        send_scales(ways[m][1], "ep", "ep", m, sem["res%d" % m])
+        send_codes(ways[m][1], "ec", "ec", m, sem["rec%d" % m])
+
     def relay_e():
-        for m in range(NT):
-            if core not in ways[m][1:-1]:
-                continue
-            k = ways[m].index(core)
+        for k, m in sorted((ways[m].index(core), m) for m in range(NT) if core in ways[m][1:-1]):
             before, after, final = ways[m][k - 1], ways[m][k + 1], k + 2 == len(ways[m])
-            rs = sem["ab%d" % m] if final else sem["re%d" % m]
-            g.wait_ge(sem["re%d" % m], 2 * (n_eng(before, core) // (NT if k == 1 else 1)))
-            send_codes(after, "bc" if final else "ec", "ec", m, rs)
-            send_scales(after, "bp" if final else "ep", "ep", m, rs)
+            g.wait_ge(sem["res%d" % m], n_eng(before, core))
+            send_scales(after, "bp" if final else "ep", "ep", m, sem["ab%d" % m] if final else sem["res%d" % m])
+            g.wait_ge(sem["rec%d" % m], n_eng(before, core))
+            send_codes(after, "bc" if final else "ec", "ec", m, sem["ab%d" % m] if final else sem["rec%d" % m])
 
     def finish():
         if left[0]:
@@ -111,18 +112,19 @@ def rank_program(g, core, T, topo):
 
     if last:
         for m in range(NT):
-            q = Y if m % 2 == 0 else S
-            q.dma_start(T.xin[:, 512 * m:512 * m + 512], T.x[:, 512 * m:512 * m + 512]).then_inc(sem["ldx%d" % m], 16)
+            Y.dma_start(T.xin[:, 512 * m:512 * m + 512], T.x[:, 512 * m:512 * m + 512]).then_inc(sem["ldx%d" % m], 16)
         for q in (Y, S):
             q.wait_ge(sem["lx"], NT * 2 * n_eng(core, R[0]))
     if rank == 0:
-        Y.dma_start(T.ein[:], T.e[:]).then_inc(sem["lde"], 16)
+        Y.dma_start(T.ein[:, 0:512], T.e[:, 0:512]).then_inc(sem["lde0"], 16)
+        Y.dma_start(T.ein[:, 512:2048], T.e[:, 512:2048]).then_inc(sem["lde1"], 16)
     (S if rank == 0 else Y).dma_start(T.win[:], T.w[:]).then_inc(sem["ldw"], 16)
     (Y if rank == 0 else S).dma_start(T.vin[:], T.v[:]).then_inc(sem["ldv"], 16)
 
     if rank == 0:
-        V.wait_ge(sem["lde"], 16)
-        V.quantize_mx(T.ec[:], T.ep[:], T.ein[:]).then_inc(sem["eq"], 1)
+        for k, a, b in ((0, 0, 1), (1, 1, NT)):
+            V.wait_ge(sem["lde%d" % k], 16)
+            V.quantize_mx(T.ec[:, W * a:W * b], T.ep[:, W * a:W * b], T.ein[:, 512 * a:512 * b]).then_inc(sem["eq"], 1)
     if last:
         for m in range(NT):
             V.wait_ge(sem["ldx%d" % m], 16)
@@ -133,20 +135,8 @@ def rank_program(g, core, T, topo):
     V.quantize_mx(T.vc[:], T.vp[:], T.vin[:]).then_inc(sem["vr"], 1)
 
     if rank == 0:
-        g.wait_ge(sem["eq"], 1)
-        eng = _bits(topo.mask(core, ways[0][1]))
-        per = len(eng) // NT
-        for buf in ("ec", "ep"):
-            tr = []
-            for m in range(NT):
-                rid, pid, _ = topo.addr(ways[m][1])
-                src, dst = T[buf][:, cols(m)], T[buf][:, cols(m)]
-                if buf == "ec":
-                    src, dst = src.bitcast(dt.uint8), dst.bitcast(dt.uint8)
-                tr.append(RemoteDMATransfer(dst_ids=[DstId(rid=rid, pnc=pid)], dma_engine_mask=sum(eng[per * m:per * m + per]),
-                                            remote_sem=sem["re%d" % m], src=src, dst=dst))
-            g.remote_dma_fused(tr, local_sem=sem["ls"])
-            left[0] += len(eng)
+        for m in (0, 2, 3):
+            start_e(m)
     if last:
         for m in range(NT):
             g.wait_ge(sem["xq"], m + 1)
@@ -162,12 +152,12 @@ def rank_program(g, core, T, topo):
     else:
         back_arrive = [2 * n_eng(R[rank + 1], core)] * NT
 
-    def mm(bk, wts, i, src, m):
-        PE.matmul_mx(T.ps[:, 512 * bk:512 * bk + W], T[wts + "c"][:, cols(i)], T[wts + "p"][:, cols(i)],
-                     T[src + "c"][:, cols(m)], T[src + "p"][:, cols(m)], True, True).then_inc(sem["pe"], 1)
+    def mm(bk, wts, i, src, m, n=1):
+        PE.matmul_mx(T.ps[:, 512 * bk:512 * bk + W * n], T[wts + "c"][:, cols(i)], T[wts + "p"][:, cols(i)],
+                     T[src + "c"][:, cols(m, n)], T[src + "p"][:, cols(m, n)], True, True).then_inc(sem["pe"], 1)
 
-    def bank(k):
-        return T.ps[:, 512 * k:512 * k + W]
+    def bank(k, m=0):
+        return T.ps[:, 512 * k + W * m:512 * k + W * m + W]
 
     def lane(buf, m, b):
         return T[buf][:, 512 * m + b:512 * m + 512:4]
@@ -177,37 +167,53 @@ def rank_program(g, core, T, topo):
 
     if last:
         PE.wait_ge(sem["vr"], 1)
-        PE.wait_ge(sem["wr"], 1)
         for m in range(NT):
             PE.wait_ge(sem["ab%d" % m], back_arrive[m])
-            if m:
-                PE.wait_ge(sem["va"], 6 * m)
-                PE.wait_ge(sem["sa"], 4 * m)
-            for i in range(4):
-                mm(4 + i, "v", i, "b", m)
+        for i in range(4):
+            mm(4 + i, "v", i, "b", 0, NT)
+        PE.wait_ge(sem["wr"], 1)
+        for m in range(NT):
+            p, v, s = 4 * m + 4, 6 * m, 4 * m
             PE.wait_ge(sem["ad%d" % m], n_down)
+            if m:
+                PE.wait_ge(sem["va"], v - 3)
+                PE.wait_ge(sem["sa"], s - 1)
             for i in range(4):
                 mm(i, "w", i, "a", m)
-            p, v, s = 8 * m + 4, 6 * m, 4 * m
             for k, b in enumerate((1, 2)):
                 S.wait_ge(sem["pe"], p + b + 1)
                 S.activation(lane("sg", m, b), bank(b), F.Sign).then_inc(sem["sa"], 1)
                 S.wait_ge(sem["sa"], s + 2 * k + 1)
                 S.activation(lane("mask", m, b), lane("sg", m, b), F.Relu, scale=C).then_inc(sem["sa"], 1)
-            for k, b in enumerate((0, 3)):
+
+            def mask(b):
                 V.wait_ge(sem["pe"], p + b + 1)
                 V.tensor_scalar(lane("mask", m, b), bank(b), 0.0, C, A.is_gt, A.mult).then_inc(sem["va"], 1)
-                V.wait_ge(sem["va"], v + 2 * k + 1)
-                V.tensor_tensor(lane("tb", m, b), bank(4 + b), lane("mask", m, b), A.mult).then_inc(sem["va"], 1)
-            for k, b in enumerate((1, 2)):
-                V.wait_ge(sem["sa"], s + 2 * k + 2)
-                V.tensor_tensor(lane("tb", m, b), bank(4 + b), lane("mask", m, b), A.mult).then_inc(sem["va"], 1)
+
+            def product(b, sm, count):
+                V.wait_ge(sem[sm], count)
+                V.tensor_tensor(lane("tb", m, b), bank(4 + b, m), lane("mask", m, b), A.mult).then_inc(sem["va"], 1)
+
+            mask(0)
+            product(0, "va", v + 1)
+            mask(3)
+            product(1, "sa", s + 2)
+            product(3, "va", v + 3)
+            product(2, "sa", s + 4)
             V.wait_ge(sem["va"], v + 6)
             quantise(m, "uc", "up", "tb")
     else:
         jobs = [("d", m) for m in range(NT)] + [("b", m) for m in range(NT)]
         va = sa = 0
+        stored = [0, 0]
         done = []
+
+        def store(k, a, b):
+            q, st = ((Y, "st0"), (S, "st1"))[k]
+            q.wait_ge(sem["va"], va)
+            q.dma_start(T.y[:, cols(a, b - a)], T.yb[:, cols(a, b - a)]).then_inc(sem[st], 16)
+            stored[k] += 16
+
         for j, (way, m) in enumerate(jobs):
             base = 4 * (j % 2)
             p = 4 * j
@@ -245,17 +251,19 @@ def rank_program(g, core, T, topo):
                     out = lane("tb", m, b) if rank else T.yb[:, cols(4 * m + b)]
                     V.tensor_tensor(out, bank(base + b), lane("mask", m, b), A.mult).then_inc(sem["va"], 1)
                     va += 1
-                    if rank == 0 and b % 2:
-                        q, st = ((Y, "st0"), (S, "st1"))[b // 2]
-                        q.wait_ge(sem["va"], va)
-                        q.dma_start(T.y[:, cols(4 * m + b - 1, 2)], T.yb[:, cols(4 * m + b - 1, 2)]).then_inc(sem[st], 16)
+                    if rank == 0:
+                        y = 4 * m + b
+                        if m == NT - 1 and b >= 2:
+                            store(3 - b, y, y + 1)
+                        elif b % 2:
+                            store(b // 2, y - 1, y + 1)
                 if rank:
                     V.wait_ge(sem["va"], va)
                     quantise(m, "uc", "up", "tb")
             done.append((va, sa))
         if rank == 0:
-            Y.wait_ge(sem["st0"], 16 * NT)
-            S.wait_ge(sem["st1"], 16 * NT)
+            Y.wait_ge(sem["st0"], stored[0])
+            S.wait_ge(sem["st1"], stored[1])
 
     n = 0
     if not last:
@@ -264,6 +272,8 @@ def rank_program(g, core, T, topo):
             g.wait_ge(sem["qz"], n)
             send_codes(R[rank + 1], "ac", "dc", m, sem["ad%d" % m])
             send_scales(R[rank + 1], "ap", "dp", m, sem["ad%d" % m])
+            if rank == 0 and m == 0:
+                start_e(1)
     if rank:
         for m in range(NT):
             n += 1

from concourse.mybir import dt, AluOpType, ActivationFunctionType

C = 0.037
NT, W, NCORES = 4, 128, 64

SCRATCH = {
    "ps": ("psum", [128, 4096], "float32"),
    "xin": ("sbuf", [128, 2048], "bfloat16"),
    "ein": ("sbuf", [128, 2048], "bfloat16"),
    "win": ("sbuf", [128, 2048], "bfloat16"),
    "vin": ("sbuf", [128, 2048], "bfloat16"),
    "wc": ("sbuf", [128, 512], "float8_e4m3fn_x4"), "wp": ("sbuf", [128, 512], "uint8"),
    "vc": ("sbuf", [128, 512], "float8_e4m3fn_x4"), "vp": ("sbuf", [128, 512], "uint8"),
    "xc": ("sbuf", [128, 512], "float8_e4m3fn_x4"), "xp": ("sbuf", [128, 512], "uint8"),
    "ec": ("sbuf", [128, 512], "float8_e4m3fn_x4"), "ep": ("sbuf", [128, 512], "uint8"),
    "ac": ("sbuf", [128, 512], "float8_e4m3fn_x4"), "ap": ("sbuf", [128, 512], "uint8"),
    "bc": ("sbuf", [128, 512], "float8_e4m3fn_x4"), "bp": ("sbuf", [128, 512], "uint8"),
    "dc": ("sbuf", [128, 512], "float8_e4m3fn_x4"), "dp": ("sbuf", [128, 512], "uint8"),
    "uc": ("sbuf", [128, 512], "float8_e4m3fn_x4"), "up": ("sbuf", [128, 512], "uint8"),
    "rc": ("sbuf", [128, 512], "float8_e4m3fn_x4"), "rp": ("sbuf", [128, 512], "uint8"),
    "td": ("sbuf", [128, 2048], "bfloat16"),
    "tb": ("sbuf", [128, 2048], "bfloat16"),
    "mask": ("sbuf", [128, 2048], "float32"),
    "sg": ("sbuf", [128, 2048], "float32"),
    "yb": ("sbuf", [128, 2048], "float32"),
}
SEMAPHORES = (["ldw", "ldv", "lde0", "lde1", "wr", "vr", "eq", "xq", "pe", "va", "sa", "qz", "mk", "ls", "lx", "st0", "st1"]
              + ["%s%d" % (k, m) for k in ("ldx", "ad", "ab", "rec", "res", "rb") for m in range(NT)])


def _bits(mask):
    return [1 << k for k in range(mask.bit_length()) if (mask >> k) & 1]


def _plan(T, topo):
    R = T.cores

    def helper(near, far, die):
        return [c for c in range(NCORES) if topo.chip(c) == topo.chip(near) and T.rank_of(c) is None
                and topo.may_write(c, far) and topo.die(c) == die][0]
    d0, d1 = topo.die(R[0]), topo.die(R[-1])
    hA, hB = helper(R[0], R[7], d0), helper(R[0], R[7], d1)
    kA, kB = helper(R[7], R[0], d0), helper(R[7], R[0], d1)
    ways = [[R[0], R[1], hA, R[5], R[7]],
            [R[0], hA, R[4], kB, R[7]],
            [R[0], R[2], hB, R[6], R[7]],
            [R[0], R[3], hB, kA, R[7]]]
    return ways, kA, kB


def rank_program(g, core, T, topo):
    A = AluOpType
    F = ActivationFunctionType
    sem = T.sem
    R = T.cores
    N = len(R)
    rank = T.rank_of(core)
    ways, kA, kB = _plan(T, topo)
    left = [0]

    def n_eng(src, dst):
        return len(_bits(topo.mask(src, dst)))

    def cols(m, n=1):
        return slice(W * m, W * (m + n))

    def send(dst, out_ap, in_ap, rsem, lsem=None):
        mask = topo.mask(core, dst)
        rid, pid, _ = topo.addr(dst)
        if lsem is None:
            lsem = sem["ls"]
            left[0] += len(_bits(mask))
        g.remote_dma(out_ap, in_ap, rsem, lsem, pid, rid, mask)

    def send_codes(dst, dbuf, sbuf, m, rsem, lsem=None):
        send(dst, T[dbuf][:, cols(m)].bitcast(dt.uint8), T[sbuf][:, cols(m)].bitcast(dt.uint8), rsem, lsem)

    def send_scales(dst, dbuf, sbuf, m, rsem, lsem=None):
        send(dst, T[dbuf][:, cols(m)], T[sbuf][:, cols(m)], rsem, lsem)

    def start_e(m):
        g.wait_ge(sem["eq"], 2 if m else 1)
        send_scales(ways[m][1], "ep", "ep", m, sem["res%d" % m])
        send_codes(ways[m][1], "ec", "ec", m, sem["rec%d" % m])

    def relay_e():
        for k, m in sorted((ways[m].index(core), m) for m in range(NT) if core in ways[m][1:-1]):
            before, after, final = ways[m][k - 1], ways[m][k + 1], k + 2 == len(ways[m])
            g.wait_ge(sem["res%d" % m], n_eng(before, core))
            send_scales(after, "bp" if final else "ep", "ep", m, sem["ab%d" % m] if final else sem["res%d" % m])
            g.wait_ge(sem["rec%d" % m], n_eng(before, core))
            send_codes(after, "bc" if final else "ec", "ec", m, sem["ab%d" % m] if final else sem["rec%d" % m])

    def finish():
        if left[0]:
            g.wait_ge(sem["ls"], left[0])

    if rank is None:
        relay_e()
        if core in (kA, kB):
            for m in range(NT):
                g.wait_ge(sem["rb%d" % m], n_eng(R[4], core))
                if core == kA:
                    send_codes(R[3], "bc", "rc", m, sem["ab%d" % m])
                else:
                    send_scales(R[3], "bp", "rp", m, sem["ab%d" % m])
        finish()
        return

    last = rank == N - 1
    PE, V, S, Y = g.tensor, g.vector, g.scalar, g.sync

    if last:
        for m in range(NT):
            Y.dma_start(T.xin[:, 512 * m:512 * m + 512], T.x[:, 512 * m:512 * m + 512]).then_inc(sem["ldx%d" % m], 16)
        for q in (Y, S):
            q.wait_ge(sem["lx"], NT * 2 * n_eng(core, R[0]))
    if rank == 0:
        Y.dma_start(T.ein[:, 0:512], T.e[:, 0:512]).then_inc(sem["lde0"], 16)
        Y.dma_start(T.ein[:, 512:2048], T.e[:, 512:2048]).then_inc(sem["lde1"], 16)
    (S if rank == 0 else Y).dma_start(T.win[:], T.w[:]).then_inc(sem["ldw"], 16)
    (Y if rank == 0 else S).dma_start(T.vin[:], T.v[:]).then_inc(sem["ldv"], 16)

    if rank == 0:
        for k, a, b in ((0, 0, 1), (1, 1, NT)):
            V.wait_ge(sem["lde%d" % k], 16)
            V.quantize_mx(T.ec[:, W * a:W * b], T.ep[:, W * a:W * b], T.ein[:, 512 * a:512 * b]).then_inc(sem["eq"], 1)
    if last:
        for m in range(NT):
            V.wait_ge(sem["ldx%d" % m], 16)
            V.quantize_mx(T.xc[:, cols(m)], T.xp[:, cols(m)], T.xin[:, 512 * m:512 * m + 512]).then_inc(sem["xq"], 1)
    V.wait_ge(sem["ldw"], 16)
    V.quantize_mx(T.wc[:], T.wp[:], T.win[:]).then_inc(sem["wr"], 1)
    V.wait_ge(sem["ldv"], 16)
    V.quantize_mx(T.vc[:], T.vp[:], T.vin[:]).then_inc(sem["vr"], 1)

    if rank == 0:
        for m in (0, 2, 3):
            start_e(m)
    if last:
        for m in range(NT):
            g.wait_ge(sem["xq"], m + 1)
            send_codes(R[0], "ac", "xc", m, sem["ad%d" % m], sem["lx"])
            send_scales(R[0], "ap", "xp", m, sem["ad%d" % m], sem["lx"])
    relay_e()

    n_down = 2 * n_eng(R[rank - 1], core)
    if last:
        back_arrive = [2 * n_eng(ways[m][-2], core) for m in range(NT)]
    elif rank == 3:
        back_arrive = [n_eng(kA, core) + n_eng(kB, core)] * NT
    else:
        back_arrive = [2 * n_eng(R[rank + 1], core)] * NT

    def mm(bk, wts, i, src, m, n=1):
        PE.matmul_mx(T.ps[:, 512 * bk:512 * bk + W * n], T[wts + "c"][:, cols(i)], T[wts + "p"][:, cols(i)],
                     T[src + "c"][:, cols(m, n)], T[src + "p"][:, cols(m, n)], True, True).then_inc(sem["pe"], 1)

    def bank(k, m=0):
        return T.ps[:, 512 * k + W * m:512 * k + W * m + W]

    def lane(buf, m, b):
        return T[buf][:, 512 * m + b:512 * m + 512:4]

    def quantise(m, codes, scales, tile):
        V.quantize_mx(T[codes][:, cols(m)], T[scales][:, cols(m)], T[tile][:, 512 * m:512 * m + 512]).then_inc(sem["qz"], 1)

    if last:
        PE.wait_ge(sem["vr"], 1)
        for m in range(NT):
            PE.wait_ge(sem["ab%d" % m], back_arrive[m])
        for i in range(4):
            mm(4 + i, "v", i, "b", 0, NT)
        PE.wait_ge(sem["wr"], 1)
        for m in range(NT):
            p, v, s = 4 * m + 4, 6 * m, 4 * m
            PE.wait_ge(sem["ad%d" % m], n_down)
            if m:
                PE.wait_ge(sem["va"], v - 3)
                PE.wait_ge(sem["sa"], s - 1)
            for i in range(4):
                mm(i, "w", i, "a", m)
            for k, b in enumerate((1, 2)):
                S.wait_ge(sem["pe"], p + b + 1)
                S.activation(lane("sg", m, b), bank(b), F.Sign).then_inc(sem["sa"], 1)
                S.wait_ge(sem["sa"], s + 2 * k + 1)
                S.activation(lane("mask", m, b), lane("sg", m, b), F.Relu, scale=C).then_inc(sem["sa"], 1)

            def mask(b):
                V.wait_ge(sem["pe"], p + b + 1)
                V.tensor_scalar(lane("mask", m, b), bank(b), 0.0, C, A.is_gt, A.mult).then_inc(sem["va"], 1)

            def product(b, sm, count):
                V.wait_ge(sem[sm], count)
                V.tensor_tensor(lane("tb", m, b), bank(4 + b, m), lane("mask", m, b), A.mult).then_inc(sem["va"], 1)

            mask(0)
            product(0, "va", v + 1)
            mask(3)
            product(1, "sa", s + 2)
            product(3, "va", v + 3)
            product(2, "sa", s + 4)
            V.wait_ge(sem["va"], v + 6)
            quantise(m, "uc", "up", "tb")
    else:
        jobs = [("d", m) for m in range(NT)] + [("b", m) for m in range(NT)]
        va = sa = 0
        stored = [0, 0]
        done = []

        def store(k, a, b):
            q, st = ((Y, "st0"), (S, "st1"))[k]
            q.wait_ge(sem["va"], va)
            q.dma_start(T.y[:, cols(a, b - a)], T.yb[:, cols(a, b - a)]).then_inc(sem[st], 16)
            stored[k] += 16

        for j, (way, m) in enumerate(jobs):
            base = 4 * (j % 2)
            p = 4 * j
            if m == 0:
                PE.wait_ge(sem["wr" if way == "d" else "vr"], 1)
            PE.wait_ge(sem["a%s%d" % (way, m)], n_down if way == "d" else back_arrive[m])
            if j >= 2:
                PE.wait_ge(sem["va"], done[j - 2][0])
                if jobs[j - 2][0] == "d":
                    PE.wait_ge(sem["sa"], done[j - 2][1])
            for i in range(4):
                mm(base + i, "w" if way == "d" else "v", i, "a" if way == "d" else "b", m)
            if way == "d":
                for b in (1, 2):
                    S.wait_ge(sem["pe"], p + b + 1)
                    S.activation(lane("td", m, b), bank(base + b), F.Relu, scale=C).then_inc(sem["sa"], 1)
                    sa += 1
                for b in (0, 3):
                    V.wait_ge(sem["pe"], p + b + 1)
                    V.tensor_scalar(lane("td", m, b), bank(base + b), 0.0, C, A.max, A.mult).then_inc(sem["va"], 1)
                    va += 1
                V.wait_ge(sem["sa"], sa)
                V.wait_ge(sem["va"], va)
                quantise(m, "dc", "dp", "td")
                t = slice(512 * m, 512 * m + 512)
                if rank == 0:
                    V.tensor_scalar(T.mask[:, t], T.td[:, t], 0.0, None, A.is_gt).then_inc(sem["mk"], 1)
                else:
                    V.tensor_scalar(T.mask[:, t], T.td[:, t], 0.0, C, A.is_gt, A.mult).then_inc(sem["mk"], 1)
            else:
                if m == 0:
                    V.wait_ge(sem["mk"], NT)
                for b in range(4):
                    V.wait_ge(sem["pe"], p + b + 1)
                    out = lane("tb", m, b) if rank else T.yb[:, cols(4 * m + b)]
                    V.tensor_tensor(out, bank(base + b), lane("mask", m, b), A.mult).then_inc(sem["va"], 1)
                    va += 1
                    if rank == 0:
                        y = 4 * m + b
                        if m == NT - 1 and b >= 2:
                            store(3 - b, y, y + 1)
                        elif b % 2:
                            store(b // 2, y - 1, y + 1)
                if rank:
                    V.wait_ge(sem["va"], va)
                    quantise(m, "uc", "up", "tb")
            done.append((va, sa))
        if rank == 0:
            Y.wait_ge(sem["st0"], stored[0])
            S.wait_ge(sem["st1"], stored[1])

    n = 0
    if not last:
        for m in range(NT):
            n += 1
            g.wait_ge(sem["qz"], n)
            send_codes(R[rank + 1], "ac", "dc", m, sem["ad%d" % m])
            send_scales(R[rank + 1], "ap", "dp", m, sem["ad%d" % m])
            if rank == 0 and m == 0:
                start_e(1)
    if rank:
        for m in range(NT):
            n += 1
            g.wait_ge(sem["qz"], n)
            if rank == 4:
                send_codes(kA, "rc", "uc", m, sem["rb%d" % m])
                send_scales(kB, "rp", "up", m, sem["rb%d" % m])
            else:
                send_codes(R[rank - 1], "bc", "uc", m, sem["ab%d" % m])
                send_scales(R[rank - 1], "bp", "up", m, sem["ab%d" % m])
    finish()
